import numpy as np
import ml_dtypes

BF16 = ml_dtypes.bfloat16


def bf(x):
    return np.asarray(x, np.float32).astype(BF16)


def f32(x):
    return np.asarray(x, np.float32)


def f64(x):
    return np.asarray(x).astype(np.float64)


def striped(idx):
    return np.tile(idx.reshape(-1, 16).T, (8, 1))


S, K, M, N, E, Q = 512, 512, 128, 384, 2, 192


def setup_inputs():
    return {"base": bf(np.random.standard_normal((M, S))), "x": bf(np.random.standard_normal((K, N))), "w": bf(np.random.standard_normal((E, K, M)) / np.sqrt(K)), "b": f32(0.5 * np.random.standard_normal((M, 1))), "offs": striped(np.random.permutation(S)[:N])}


def reference(base, x, w, b, offs):
    idx = offs[:16].T.reshape(-1)
    z = f64(base).copy()
    for e in range(E):
        z[:, idx[e * Q : (e + 1) * Q]] += f64(w)[e].T @ f64(x)[:, e * Q : (e + 1) * Q]
    return np.maximum(z + f64(b), 0.0)

@@ -1,0 +1,58 @@
+import concourse.mybir as mybir
+from concourse.masks import make_identity
+
+BF16, F32, U16 = mybir.dt.bfloat16, mybir.dt.float32, mybir.dt.uint16
+RELU = mybir.ActivationFunctionType.Relu
+
+P = 128
+TOKENS = 512
+K = 512
+K_BLOCKS = K // P
+EXPERTS = 2
+PIECE = 192
+ENTRIES = EXPERTS * PIECE
+PIECE_COLS = PIECE // 16
+
+FLOPS = 2 * K * P * ENTRIES
+
+
+def tile_scatter_matmul_kernel(tc, base, x, w, b, offs, out):
+    nc = tc.nc
+    with (
+        tc.tile_pool(name="held", bufs=1) as held,
+        tc.psum_pool(name="psum", bufs=1) as psum,
+    ):
+        offsets = held.tile([P, ENTRIES // 16], U16, name="offsets")
+        nc.sync.dma_start(offsets[:], offs)
+
+        base_tile = held.tile([P, TOKENS], BF16, name="base_tile")
+        nc.scalar.dma_start(base_tile[:], base)
+        bias = held.tile([P, 1], F32, name="bias")
+        nc.scalar.dma_start(bias[:], b)
+
+        x_tile = held.tile([P, K_BLOCKS, ENTRIES], BF16, name="x_tile")
+        nc.sync.dma_start(x_tile[:], x.rearrange("(kb p) n -> p kb n", p=P))
+        w_tile = held.tile([P, EXPERTS * K_BLOCKS, P], BF16, name="w_tile")
+        nc.scalar.dma_start(w_tile[:], w.rearrange("e (kb p) m -> p (e kb) m", p=P))
+
+        identity = held.tile([P, P], BF16, name="identity")
+        make_identity(nc, identity[:])
+
+        window = psum.tile([P, TOKENS], F32, name="window")
+        nc.tensor.matmul(window[:], identity[:], base_tile[:], start=True, stop=False)
+
+        for e in range(EXPERTS):
+            piece = offsets[:, e * PIECE_COLS : (e + 1) * PIECE_COLS]
+            for kb in range(K_BLOCKS):
+                last = e == EXPERTS - 1 and kb == K_BLOCKS - 1
+                nc.tensor.matmul(
+                    window[:].indirect(piece),
+                    w_tile[:, e * K_BLOCKS + kb, :],
+                    x_tile[:, kb, e * PIECE : (e + 1) * PIECE],
+                    start=False,
+                    stop=last,
+                )
+
+        result = held.tile([P, TOKENS], F32, name="result")
+        nc.scalar.activation(result[:], window[:], RELU, bias=bias[:])
+        nc.sync.dma_start(out, result[:])

@@ -7,7 +7,8 @@ RELU = mybir.ActivationFunctionType.Relu
 P = 128
 TOKENS = 512
 K = 512
-K_BLOCKS = K // P
+STEPS = K // P
+HALF = STEPS // 2
 EXPERTS = 2
 PIECE = 192
 ENTRIES = EXPERTS * PIECE
@@ -27,30 +28,33 @@ def tile_scatter_matmul_kernel(tc, base, x, w, b, offs, out):
 
         base_tile = held.tile([P, TOKENS], BF16, name="base_tile")
         nc.scalar.dma_start(base_tile[:], base)
-        bias = held.tile([P, 1], F32, name="bias")
-        nc.scalar.dma_start(bias[:], b)
 
-        x_tile = held.tile([P, K_BLOCKS, ENTRIES], BF16, name="x_tile")
-        nc.sync.dma_start(x_tile[:], x.rearrange("(kb p) n -> p kb n", p=P))
-        w_tile = held.tile([P, EXPERTS * K_BLOCKS, P], BF16, name="w_tile")
-        nc.scalar.dma_start(w_tile[:], w.rearrange("e (kb p) m -> p (e kb) m", p=P))
+        x_rows = x.rearrange("(p s) n -> p s n", s=STEPS)
+        w_rows = w.rearrange("e (p s) m -> p e s m", s=STEPS)
+        x_half, w_half = [], []
+        for h in range(STEPS // HALF):
+            steps = slice(h * HALF, (h + 1) * HALF)
+            x_half.append(held.tile([P, HALF, ENTRIES], BF16, name="x_half%d" % h))
+            nc.sync.dma_start(x_half[h][:], x_rows[:, steps, :])
+            w_half.append(held.tile([P, EXPERTS, HALF, P], BF16, name="w_half%d" % h))
+            nc.scalar.dma_start(w_half[h][:], w_rows[:, :, steps, :])
 
         identity = held.tile([P, P], BF16, name="identity")
         make_identity(nc, identity[:])
+        bias = held.tile([P, 1], F32, name="bias")
+        nc.gpsimd.dma_start(bias[:], b)
 
         window = psum.tile([P, TOKENS], F32, name="window")
         nc.tensor.matmul(window[:], identity[:], base_tile[:], start=True, stop=False)
 
-        for e in range(EXPERTS):
-            piece = offsets[:, e * PIECE_COLS : (e + 1) * PIECE_COLS]
-            for kb in range(K_BLOCKS):
-                last = e == EXPERTS - 1 and kb == K_BLOCKS - 1
+        for s in range(STEPS):
+            for e in range(EXPERTS):
                 nc.tensor.matmul(
-                    window[:].indirect(piece),
-                    w_tile[:, e * K_BLOCKS + kb, :],
-                    x_tile[:, kb, e * PIECE : (e + 1) * PIECE],
+                    window[:].indirect(offsets[:, e * PIECE_COLS : (e + 1) * PIECE_COLS]),
+                    w_half[s // HALF][:, e, s % HALF, :],
+                    x_half[s // HALF][:, s % HALF, e * PIECE : (e + 1) * PIECE],
                     start=False,
-                    stop=last,
+                    stop=(s == STEPS - 1 and e == EXPERTS - 1),
                 )
 
         result = held.tile([P, TOKENS], F32, name="result")

@@ -13,6 +13,7 @@ EXPERTS = 2
 PIECE = 192
 ENTRIES = EXPERTS * PIECE
 PIECE_COLS = PIECE // 16
+WARM_UPS = 16
 
 FLOPS = 2 * K * P * ENTRIES
 
@@ -23,6 +24,12 @@ def tile_scatter_matmul_kernel(tc, base, x, w, b, offs, out):
         tc.tile_pool(name="held", bufs=1) as held,
         tc.psum_pool(name="psum", bufs=1) as psum,
     ):
+        zeros = held.tile([P, P], BF16, name="zeros")
+        nc.vector.memset(zeros[:], 0.0)
+        unread = psum.tile([P, P], F32, name="unread")
+        for i in range(WARM_UPS):
+            nc.tensor.matmul(unread[:], zeros[:], zeros[:], start=True, stop=True)
+
         offsets = held.tile([P, ENTRIES // 16], U16, name="offsets")
         nc.sync.dma_start(offsets[:], offs)
 

@@ -2,7 +2,7 @@ import concourse.mybir as mybir
 from concourse.masks import make_identity
 
 BF16, F32, U16 = mybir.dt.bfloat16, mybir.dt.float32, mybir.dt.uint16
-RELU = mybir.ActivationFunctionType.Relu
+ADD, MAX = mybir.AluOpType.add, mybir.AluOpType.max
 
 P = 128
 TOKENS = 512
@@ -45,11 +45,11 @@ def tile_scatter_matmul_kernel(tc, base, x, w, b, offs, out):
             nc.sync.dma_start(x_half[h][:], x_rows[:, steps, :])
             w_half.append(held.tile([P, EXPERTS, HALF, P], BF16, name="w_half%d" % h))
             nc.scalar.dma_start(w_half[h][:], w_rows[:, :, steps, :])
+        bias = held.tile([P, 1], F32, name="bias")
+        nc.scalar.dma_start(bias[:], b)
 
         identity = held.tile([P, P], BF16, name="identity")
         make_identity(nc, identity[:])
-        bias = held.tile([P, 1], F32, name="bias")
-        nc.gpsimd.dma_start(bias[:], b)
 
         window = psum.tile([P, TOKENS], F32, name="window")
         nc.tensor.matmul(window[:], identity[:], base_tile[:], start=True, stop=False)
@@ -65,5 +65,7 @@ def tile_scatter_matmul_kernel(tc, base, x, w, b, offs, out):
                 )
 
         result = held.tile([P, TOKENS], F32, name="result")
-        nc.scalar.activation(result[:], window[:], RELU, bias=bias[:])
-        nc.sync.dma_start(out, result[:])
+        for c, queue in enumerate((nc.sync, nc.scalar)):
+            cols = slice(c * TOKENS // 2, (c + 1) * TOKENS // 2)
+            nc.vector.tensor_scalar(result[:, cols], window[:, cols], bias[:], 0.0, op0=ADD, op1=MAX)
+            queue.dma_start(out[:, cols], result[:, cols])

@@ -8,7 +8,6 @@ P = 128
 TOKENS = 512
 K = 512
 STEPS = K // P
-HALF = STEPS // 2
 EXPERTS = 2
 PIECE = 192
 ENTRIES = EXPERTS * PIECE
@@ -36,15 +35,14 @@ def tile_scatter_matmul_kernel(tc, base, x, w, b, offs, out):
         base_tile = held.tile([P, TOKENS], BF16, name="base_tile")
         nc.scalar.dma_start(base_tile[:], base)
 
-        x_rows = x.rearrange("(p s) n -> p s n", s=STEPS)
-        w_rows = w.rearrange("e (p s) m -> p e s m", s=STEPS)
-        x_half, w_half = [], []
-        for h in range(STEPS // HALF):
-            steps = slice(h * HALF, (h + 1) * HALF)
-            x_half.append(held.tile([P, HALF, ENTRIES], BF16, name="x_half%d" % h))
-            nc.sync.dma_start(x_half[h][:], x_rows[:, steps, :])
-            w_half.append(held.tile([P, EXPERTS, HALF, P], BF16, name="w_half%d" % h))
-            nc.scalar.dma_start(w_half[h][:], w_rows[:, :, steps, :])
+        x_rows = x.rearrange("(s p) n -> s p n", p=P)
+        w_rows = w.rearrange("e (s p) m -> s p e m", p=P)
+        x_step, w_step = [], []
+        for s in range(STEPS):
+            x_step.append(held.tile([P, ENTRIES], BF16, name="x_step%d" % s))
+            nc.sync.dma_start(x_step[s][:], x_rows[s])
+            w_step.append(held.tile([P, EXPERTS, P], BF16, name="w_step%d" % s))
+            nc.scalar.dma_start(w_step[s][:], w_rows[s])
         bias = held.tile([P, 1], F32, name="bias")
         nc.scalar.dma_start(bias[:], b)
 
@@ -58,8 +56,8 @@ def tile_scatter_matmul_kernel(tc, base, x, w, b, offs, out):
             for e in range(EXPERTS):
                 nc.tensor.matmul(
                     window[:].indirect(offsets[:, e * PIECE_COLS : (e + 1) * PIECE_COLS]),
-                    w_half[s // HALF][:, e, s % HALF, :],
-                    x_half[s // HALF][:, s % HALF, e * PIECE : (e + 1) * PIECE],
+                    w_step[s][:, e, :],
+                    x_step[s][:, e * PIECE : (e + 1) * PIECE],
                     start=False,
                     stop=(s == STEPS - 1 and e == EXPERTS - 1),
                 )

@@ -35,14 +35,25 @@ def tile_scatter_matmul_kernel(tc, base, x, w, b, offs, out):
         base_tile = held.tile([P, TOKENS], BF16, name="base_tile")
         nc.scalar.dma_start(base_tile[:], base)
 
-        x_rows = x.rearrange("(s p) n -> s p n", p=P)
-        w_rows = w.rearrange("e (s p) m -> s p e m", p=P)
+        x_early = x[0 : 2 * P, :].rearrange("(s p) n -> s p n", p=P)
+        w_early = w[:, 0 : 2 * P, :].rearrange("e (s p) m -> s p e m", p=P)
+        x_late = x[2 * P : K, :].rearrange("(p t) n -> t p n", t=2)
+        w_late = w[:, 2 * P : K, :].rearrange("e (p t) m -> p e t m", t=2)
         x_step, w_step = [], []
-        for s in range(STEPS):
-            x_step.append(held.tile([P, ENTRIES], BF16, name="x_step%d" % s))
-            nc.sync.dma_start(x_step[s][:], x_rows[s])
-            w_step.append(held.tile([P, EXPERTS, P], BF16, name="w_step%d" % s))
-            nc.scalar.dma_start(w_step[s][:], w_rows[s])
+        for s in range(2):
+            x_tile = held.tile([P, ENTRIES], BF16, name="x_tile%d" % s)
+            nc.sync.dma_start(x_tile[:], x_early[s])
+            w_tile = held.tile([P, EXPERTS, P], BF16, name="w_tile%d" % s)
+            nc.scalar.dma_start(w_tile[:], w_early[s])
+            x_step.append(x_tile[:])
+            w_step.append(w_tile[:])
+        w_pair = held.tile([P, EXPERTS, 2, P], BF16, name="w_pair")
+        nc.scalar.dma_start(w_pair[:], w_late)
+        for t in range(2):
+            x_tile = held.tile([P, ENTRIES], BF16, name="x_tile%d" % (2 + t))
+            nc.sync.dma_start(x_tile[:], x_late[t])
+            x_step.append(x_tile[:])
+            w_step.append(w_pair[:, :, t, :])
         bias = held.tile([P, 1], F32, name="bias")
         nc.scalar.dma_start(bias[:], b)
 

@@ -33,16 +33,16 @@ def tile_scatter_matmul_kernel(tc, base, x, w, b, offs, out):
         nc.sync.dma_start(offsets[:], offs)
 
         base_tile = held.tile([P, TOKENS], BF16, name="base_tile")
-        nc.scalar.dma_start(base_tile[:], base)
+        nc.sync.dma_start(base_tile[:], base)
 
         x_early = x[0 : 2 * P, :].rearrange("(s p) n -> s p n", p=P)
         w_early = w[:, 0 : 2 * P, :].rearrange("e (s p) m -> s p e m", p=P)
         x_late = x[2 * P : K, :].rearrange("(p t) n -> t p n", t=2)
         w_late = w[:, 2 * P : K, :].rearrange("e (p t) m -> p e t m", t=2)
         x_step, w_step = [], []
-        for s in range(2):
+        for s, x_queue in enumerate((nc.scalar, nc.sync)):
             x_tile = held.tile([P, ENTRIES], BF16, name="x_tile%d" % s)
-            nc.sync.dma_start(x_tile[:], x_early[s])
+            x_queue.dma_start(x_tile[:], x_early[s])
             w_tile = held.tile([P, EXPERTS, P], BF16, name="w_tile%d" % s)
             nc.scalar.dma_start(w_tile[:], w_early[s])
             x_step.append(x_tile[:])

@@ -29,11 +29,11 @@ def tile_scatter_matmul_kernel(tc, base, x, w, b, offs, out):
         for i in range(WARM_UPS):
             nc.tensor.matmul(unread[:], zeros[:], zeros[:], start=True, stop=True)
 
-        offsets = held.tile([P, ENTRIES // 16], U16, name="offsets")
-        nc.sync.dma_start(offsets[:], offs)
-
         base_tile = held.tile([P, TOKENS], BF16, name="base_tile")
         nc.sync.dma_start(base_tile[:], base)
+
+        offsets = held.tile([P, ENTRIES // 16], U16, name="offsets")
+        nc.sync.dma_start(offsets[:], offs)
 
         x_early = x[0 : 2 * P, :].rearrange("(s p) n -> s p n", p=P)
         w_early = w[:, 0 : 2 * P, :].rearrange("e (s p) m -> s p e m", p=P)

import concourse.mybir as mybir
from concourse.masks import make_identity

BF16, F32, U16 = mybir.dt.bfloat16, mybir.dt.float32, mybir.dt.uint16
ADD, MAX = mybir.AluOpType.add, mybir.AluOpType.max

P = 128
TOKENS = 512
K = 512
STEPS = K // P
EXPERTS = 2
PIECE = 192
ENTRIES = EXPERTS * PIECE
PIECE_COLS = PIECE // 16
WARM_UPS = 16

FLOPS = 2 * K * P * ENTRIES


def tile_scatter_matmul_kernel(tc, base, x, w, b, offs, out):
    nc = tc.nc
    with (
        tc.tile_pool(name="held", bufs=1) as held,
        tc.psum_pool(name="psum", bufs=1) as psum,
    ):
        zeros = held.tile([P, P], BF16, name="zeros")
        nc.vector.memset(zeros[:], 0.0)
        unread = psum.tile([P, P], F32, name="unread")
        for i in range(WARM_UPS):
            nc.tensor.matmul(unread[:], zeros[:], zeros[:], start=True, stop=True)

        base_tile = held.tile([P, TOKENS], BF16, name="base_tile")
        nc.sync.dma_start(base_tile[:], base)

        offsets = held.tile([P, ENTRIES // 16], U16, name="offsets")
        nc.sync.dma_start(offsets[:], offs)

        x_early = x[0 : 2 * P, :].rearrange("(s p) n -> s p n", p=P)
        w_early = w[:, 0 : 2 * P, :].rearrange("e (s p) m -> s p e m", p=P)
        x_late = x[2 * P : K, :].rearrange("(p t) n -> t p n", t=2)
        w_late = w[:, 2 * P : K, :].rearrange("e (p t) m -> p e t m", t=2)
        x_step, w_step = [], []
        for s, x_queue in enumerate((nc.scalar, nc.sync)):
            x_tile = held.tile([P, ENTRIES], BF16, name="x_tile%d" % s)
            x_queue.dma_start(x_tile[:], x_early[s])
            w_tile = held.tile([P, EXPERTS, P], BF16, name="w_tile%d" % s)
            nc.scalar.dma_start(w_tile[:], w_early[s])
            x_step.append(x_tile[:])
            w_step.append(w_tile[:])
        w_pair = held.tile([P, EXPERTS, 2, P], BF16, name="w_pair")
        nc.scalar.dma_start(w_pair[:], w_late)
        for t in range(2):
            x_tile = held.tile([P, ENTRIES], BF16, name="x_tile%d" % (2 + t))
            nc.sync.dma_start(x_tile[:], x_late[t])
            x_step.append(x_tile[:])
            w_step.append(w_pair[:, :, t, :])
        bias = held.tile([P, 1], F32, name="bias")
        nc.scalar.dma_start(bias[:], b)

        identity = held.tile([P, P], BF16, name="identity")
        make_identity(nc, identity[:])

        window = psum.tile([P, TOKENS], F32, name="window")
        nc.tensor.matmul(window[:], identity[:], base_tile[:], start=True, stop=False)

        for s in range(STEPS):
            for e in range(EXPERTS):
                nc.tensor.matmul(
                    window[:].indirect(offsets[:, e * PIECE_COLS : (e + 1) * PIECE_COLS]),
                    w_step[s][:, e, :],
                    x_step[s][:, e * PIECE : (e + 1) * PIECE],
                    start=False,
                    stop=(s == STEPS - 1 and e == EXPERTS - 1),
                )

        result = held.tile([P, TOKENS], F32, name="result")
        for c, queue in enumerate((nc.sync, nc.scalar)):
            cols = slice(c * TOKENS // 2, (c + 1) * TOKENS // 2)
            nc.vector.tensor_scalar(result[:, cols], window[:, cols], bias[:], 0.0, op0=ADD, op1=MAX)
            queue.dma_start(out[:, cols], result[:, cols])
